import numpy as np
import ml_dtypes


def mxq(x, axis, fmt="e4m3"):
    dtype, down = {"e4m3": (ml_dtypes.float8_e4m3fn, 7), "e5m2": (ml_dtypes.float8_e5m2, 14)}[fmt]
    v = np.moveaxis(np.asarray(x, np.float32).astype(ml_dtypes.bfloat16).astype(np.float64), axis, -1)
    blocks = v.reshape(v.shape[:-1] + (-1, 32))
    amax = np.abs(blocks).max(-1, keepdims=True)
    byte = np.maximum(np.where(amax > 0, np.frexp(amax)[1] - 1 + 127, 0) - down, 1)
    scale = np.exp2(byte - 127.0)
    codes = (blocks / scale).astype(np.float32).astype(dtype).astype(np.float64)
    return np.moveaxis((codes * scale).reshape(v.shape), -1, axis)


WIDE = False


def mx_kscale(k):
    if not WIDE:
        return np.ones(k)
    levels = np.array([10, -10, 5, -5, 0])
    if k % 512:
        return np.exp2(np.random.permutation(np.resize(levels, k // 32))).repeat(32)
    a = np.empty((k // 512, 16))
    for p in range(k // 512):
        a[p, :8] = np.random.permutation(np.resize(levels, 8))
        for g in range(8):
            far = levels[np.abs(levels - a[p, g]) >= 10]
            a[p, g + 8] = far[np.random.randint(len(far))]
    return np.exp2(a.ravel()).repeat(32)


BF16 = ml_dtypes.bfloat16


def bf(x):
    return np.asarray(x, np.float32).astype(BF16)


def f64(x):
    return np.asarray(x).astype(np.float64)

E4M3FN = np.array([(-1.0 if i & 128 else 1.0) * ((1.0 + (i & 7) / 8.0) * 2.0 ** (((i >> 3) & 15) - 7) if i & 120 else (i & 7) * 2.0 ** -9) for i in range(256)])


def e4m3fn_bytes(y):
    return np.clip(np.asarray(y, np.float64), -448.0, 448.0).astype(np.float32).astype(ml_dtypes.float8_e4m3fn).view(np.uint8)


def e4m3fn_values(b):
    return E4M3FN[b]


Q, K, P, S, BLK = 1024, 512, 2048, 1536, 128


def setup_inputs():
    s, t = mx_kscale(K), mx_kscale(P)
    w1 = np.random.standard_normal((K, P)) / np.sqrt(K) / s[:, None]
    branch = 1.5 * np.random.standard_normal((S, P)) / np.sqrt(P) / t
    d = {"y": bf(np.random.standard_normal((Q, K)) * s),
         "b1": bf(0.3 * np.random.standard_normal(P)),
         "g": bf((1 + 0.1 * np.random.standard_normal(P)) * t),
         "c": bf(0.3 * np.random.standard_normal(S))}
    for name, w in (("w1", w1), ("branch", branch)):
        rows, cols = w.shape
        sc = (np.abs(w).reshape(rows // BLK, BLK, cols // BLK, BLK).max((1, 3)) / 448).astype(np.float32)
        d[name + "_bytes"] = e4m3fn_bytes(w / np.repeat(np.repeat(f64(sc), BLK, 0), BLK, 1))
        d[name + "_scale"] = sc
    return d


def reference(y, w1_bytes, w1_scale, b1, g, branch_bytes, branch_scale, c):
    w1 = e4m3fn_values(w1_bytes) * np.repeat(np.repeat(f64(w1_scale), BLK, 0), BLK, 1)
    branch = e4m3fn_values(branch_bytes) * np.repeat(np.repeat(f64(branch_scale), BLK, 0), BLK, 1)
    h = mxq(f64(y), 1, "e4m3") @ mxq(w1, 0, "e4m3")
    basis = np.tanh(h + f64(b1)) * f64(g)
    u = mxq(branch, 1, "e4m3") @ mxq(basis, 1, "e4m3").T
    return u + f64(c)[:, None]

@@ -1,0 +1,270 @@
+from contextlib import ExitStack
+
+import concourse.mybir as mybir
+from concourse.masks import make_identity
+
+Q, K, NB, S = 1024, 512, 2048, 1536
+FLOPS = 2 * Q * K * NB + 2 * S * Q * NB
+
+F32 = mybir.dt.float32
+BF16 = mybir.dt.bfloat16
+U32 = mybir.dt.uint32
+U8 = mybir.dt.uint8
+E4M3 = mybir.dt.float8_e4m3fn
+FP8X4 = mybir.dt.float8_e4m3fn_x4
+ADD = mybir.AluOpType.add
+MULT = mybir.AluOpType.mult
+ACT = mybir.ActivationFunctionType
+
+
+CH = ((0, 512), (512, 256), (768, 256))
+WIDE_S = {0: 16, 1: 16, 2: 16, 3: 16}
+W1_S = ()
+INTER_S = ()
+EXIT_V = ()
+OUT_V = ()
+ONEPASS = False
+CONTIG = True
+WIDE_BUFS = 4
+TH_BUFS = 3
+RES_BUFS = 6
+NTR, NH, NACC = 2, 3, 3
+MANUAL = False
+ORDER = [('W', 0), ('Y', 0), ('B', 0, 0), ('W', 1), ('D', 0), ('B', 1, 0), ('W', 2), ('D', 1), ('B', 2, 0), ('W', 3), ('D', 2), ('B', 3, 0), ('N', 0), ('P', 0, 0), ('N', 1), ('P', 1, 0), ('D', 3), ('N', 2), ('P', 2, 0), ('D', 4), ('N', 3), ('P', 3, 0), ('D', 5), ('N', 4), ('P', 4, 0), ('Y', 1), ('B', 0, 1), ('D', 6), ('N', 5), ('P', 5, 0), ('B', 1, 1), ('D', 7), ('N', 6), ('P', 6, 0), ('B', 2, 1), ('D', 8), ('N', 7), ('P', 7, 0), ('B', 3, 1), ('P', 0, 1), ('P', 1, 1), ('P', 2, 1), ('D', 9), ('N', 8), ('P', 8, 0), ('Y', 2), ('B', 0, 2), ('P', 3, 1), ('P', 4, 1), ('P', 5, 1), ('D', 10), ('N', 9), ('P', 9, 0), ('B', 1, 2), ('P', 6, 1), ('P', 7, 1), ('P', 8, 1), ('D', 11), ('N', 10), ('P', 10, 0), ('B', 2, 2), ('P', 9, 1), ('P', 10, 1), ('N', 11), ('P', 11, 0), ('B', 3, 2), ('P', 11, 1), ('P', 0, 2), ('P', 1, 2), ('P', 2, 2), ('P', 3, 2), ('P', 4, 2), ('P', 5, 2), ('P', 6, 2), ('P', 7, 2), ('P', 8, 2), ('P', 9, 2), ('P', 10, 2), ('P', 11, 2)]
+
+
+def tile_operator_net_trunk_branch_d7_kernel(tc, y, b1, gain, c, w1_bytes, w1_scale, branch_bytes, branch_scale, out):
+    nc = tc.nc
+    with ExitStack() as ctx:
+        keep = ctx.enter_context(tc.tile_pool(name="keep", bufs=1))
+        work = ctx.enter_context(tc.tile_pool(name="work", bufs=2))
+        ps_tr = ctx.enter_context(tc.psum_pool(name="ps_tr", bufs=NTR))
+        ps_h = ctx.enter_context(tc.psum_pool(name="ps_h", bufs=NH))
+        ps_acc = ctx.enter_context(tc.psum_pool(name="ps_acc", bufs=NACC))
+
+        w1_raw = []
+        for g in range(4):
+            w1_raw.append(keep.tile([128, 4, 512], U8, name=f"w1_raw{g}", align_bytes=64))
+        y_sb = []
+        for h in range(2):
+            y_sb.append(keep.tile([128, 4, 512], BF16, name=f"y_sb{h}", align_bytes=64))
+        br_raw = []
+        for d in range(6):
+            br_raw.append(keep.tile([128, 2, 2048], U8, name=f"br_raw{d}", align_bytes=64))
+        w1_sc = keep.tile([128, 16], F32, name="w1_sc")
+        br_sc = keep.tile([128, 3, 16], F32, name="br_sc")
+        b1_bf = keep.tile([128, 4, 4], BF16, name="b1_bf")
+        gain_bf = keep.tile([128, 4, 4], BF16, name="gain_bf")
+        c_bf = keep.tile([128, 3, 4], BF16, name="c_bf")
+
+        w1_view = w1_bytes.rearrange("(p k) n -> p k n", k=4)
+        y_view = y.rearrange("(h i p) k -> h p i k", h=2, p=128)
+        br_view = branch_bytes.rearrange("(c p d r) k -> c d p r k", c=3, d=2, r=2)
+
+        def load_w1(g):
+            nc.sync.dma_start(out=w1_raw[g][:], in_=w1_view[:, :, 512 * g : 512 * g + 512])
+
+        ident = keep.tile([128, 128], F32, name="ident", align_bytes=64)
+        make_identity(nc, ident[:])
+        warm = keep.tile([128, 1], F32, name="warm")
+        nc.vector.memset(warm[:], 0.0)
+
+        for q in range(4):
+            nc.scalar.dma_start(out=w1_sc[32 * q : 32 * q + 32, :], in_=w1_scale[q].partition_broadcast(32))
+        load_w1(0)
+        nc.sync.dma_start(out=y_sb[0][:], in_=y_view[0])
+        nc.scalar.activation(out=warm[:], in_=warm[:], func=ACT.Tanh)
+        load_w1(1)
+        nc.sync.dma_start(out=b1_bf[:], in_=b1.rearrange("(g p t) -> p g t", g=4, t=4))
+        nc.sync.dma_start(out=gain_bf[:], in_=gain.rearrange("(g p t) -> p g t", g=4, t=4))
+        scale_view = branch_scale.rearrange("(c q) j -> q c j", q=4)
+        for q in range(4):
+            nc.gpsimd.dma_start(out=br_sc[32 * q : 32 * q + 32, :, :], in_=scale_view[q].partition_broadcast(32))
+        nc.gpsimd.dma_start(out=c_bf[:], in_=c.rearrange("(c p r) -> p c r", c=3, r=4))
+        nc.sync.dma_start(out=br_raw[0][:], in_=br_view[0, 0])
+        load_w1(2)
+        load_w1(3)
+        nc.sync.dma_start(out=y_sb[1][:], in_=y_view[1])
+        for d in range(1, 6):
+            nc.sync.dma_start(out=br_raw[d][:], in_=br_view[d // 2, d % 2])
+
+        w1_codes = [keep.tile([128, 512], U32, name=f"w1_codes{g}", align_bytes=64) for g in range(4)]
+        w1_scl = [keep.tile([128, 512], U8, name=f"w1_scl{g}", align_bytes=64) for g in range(4)]
+        y_codes = [keep.tile([128, w], U32, name=f"y_codes{h}", align_bytes=64) for h, (s, w) in enumerate(CH)]
+        y_scl = [keep.tile([128, w], U8, name=f"y_scl{h}", align_bytes=64) for h, (s, w) in enumerate(CH)]
+        ba_codes = [[keep.tile([128, w], U32, name=f"ba_codes{g}_{h}", align_bytes=64) for h, (s, w) in enumerate(CH)] for g in range(4)]
+        ba_scl = [[keep.tile([128, w], U8, name=f"ba_scl{g}_{h}", align_bytes=64) for h, (s, w) in enumerate(CH)] for g in range(4)]
+        br_codes = [keep.tile([128, 512], U32, name=f"br_codes{n}", align_bytes=64) for n in range(12)]
+        br_scl = [keep.tile([128, 512], U8, name=f"br_scl{n}", align_bytes=64) for n in range(12)]
+        st = {}
+
+        def quantize(codes, scl, src):
+            nc.vector.quantize_mx(out=codes[:].bitcast(FP8X4), scales=scl[:], in_=src)
+
+        def w1_move(g):
+            inter = work.tile([128, 4, 4, 32, 4], U8, name="w1_inter", align_bytes=64)
+            src = w1_raw[g][:].rearrange("p k (j m t) -> p j t m k", j=4, t=4)
+            for j in range(4):
+                nc.vector.tensor_copy(out=inter[:, j], in_=src[:, j])
+            st["wi", g] = inter
+
+        def w1_widen(g):
+            inter = st["wi", g]
+            wide = work.tile([128, 2048], BF16, name="w1_wide", align_bytes=64)
+            dst = wide[:].rearrange("p (t j x) -> p j t x", t=4, j=4)
+            for j in range(4):
+                fp8 = inter[:, j].rearrange("p t m k -> p t (m k)").bitcast(E4M3)
+                scale = w1_sc[:, 4 * g + j : 4 * g + j + 1]
+                if g in W1_S:
+                    for t in range(4):
+                        nc.scalar.activation(out=dst[:, j, t], in_=fp8[:, t], func=ACT.Copy, scale=scale)
+                else:
+                    nc.vector.tensor_scalar(out=dst[:, j], in0=fp8, scalar1=scale, scalar2=None, op0=MULT)
+            st["ww", g] = wide
+
+        def w1_quant(g):
+            quantize(w1_codes[g], w1_scl[g], st["ww", g][:])
+
+        def turn(words, dst_words, contiguous, on_vector):
+            for b in range(words.shape[1] // 512):
+                bank = ps_tr.tile([128, 4, 128], F32, name="tr")
+                for i in range(2):
+                    base = 256 * (2 * b + i)
+                    for u in range(2):
+                        src = words[:, base + 128 * u : base + 128 * u + 128] if contiguous else words[:, base + u : base + 256 : 2]
+                        nc.tensor.transpose(bank[:, 2 * i + u, :], src, ident[:])
+                o = dst_words[:, 512 * b : 512 * b + 512].rearrange("p (i r u) -> p i r u", i=2, u=2)
+                s = bank[:].rearrange("p (i u) r -> p i r u", i=2)
+                if on_vector:
+                    nc.vector.tensor_copy(out=o, in_=s)
+                else:
+                    nc.scalar.copy(out=o, in_=s)
+
+        def y_turn(h):
+            s, w = CH[h]
+            words = y_sb[s // 512][:, (s % 512) // 128 : (s % 512 + w) // 128].rearrange("p i k -> p (i k)").bitcast(F32)
+            grp = work.tile([128, 2048], BF16, name="y_grp", align_bytes=64)
+            turn(words, grp[:, : 4 * w].bitcast(F32), False, ("y", h) in EXIT_V)
+            st["yg", h] = grp
+
+        def y_quant(h):
+            quantize(y_codes[h], y_scl[h], st["yg", h][:, : 4 * CH[h][1]])
+
+        def basis_h(g, h):
+            s, w = CH[h]
+            th = work.tile([128, 4, 512], F32, name="th", align_bytes=64, bufs=TH_BUFS)
+            for t in range(4):
+                acc = ps_h.tile([128, 512], F32, name="h_ps")
+                cols = slice(128 * t, 128 * t + 128)
+                nc.tensor.matmul_mx(
+                    out=acc[:, :w],
+                    lhsT=w1_codes[g][:, cols].bitcast(FP8X4),
+                    lhsT_scale=w1_scl[g][:, cols],
+                    rhs=y_codes[h][:].bitcast(FP8X4),
+                    rhs_scale=y_scl[h][:],
+                    start=True,
+                    stop=True,
+                )
+                nc.scalar.activation(out=th[:, t, :w], in_=acc[:, :w], func=ACT.Tanh, bias=b1_bf[:, g, t : t + 1])
+            st["th", g, h] = th
+
+        def basis_gain(g, h):
+            s, w = CH[h]
+            th = st["th", g, h]
+            if ONEPASS:
+                grp = work.tile([128, 512, 4], BF16, name="ba_grp", align_bytes=64)
+                nc.vector.tensor_tensor(
+                    out=grp[:, :w], in0=th[:, :, :w].rearrange("p t n -> p n t"),
+                    in1=gain_bf[:, g, :].unsqueeze(1).to_broadcast([128, w, 4]), op=MULT)
+                st["bg", g, h] = grp
+                return
+            planes = work.tile([128, 4, 512], BF16, name="planes", align_bytes=64)
+            for t in range(4):
+                nc.vector.tensor_scalar(
+                    out=planes[:, t, :w], in0=th[:, t, :w], scalar1=gain_bf[:, g, t : t + 1], scalar2=None, op0=MULT
+                )
+            st["bp", g, h] = planes
+
+        def basis_inter(g, h):
+            if ONEPASS:
+                return
+            s, w = CH[h]
+            grp = work.tile([128, 512, 4], BF16, name="ba_grp", align_bytes=64)
+            o, i = grp[:, :w], st["bp", g, h][:, :, :w].rearrange("p t n -> p n t")
+            if (g, h) in INTER_S:
+                nc.scalar.copy(out=o, in_=i)
+            else:
+                nc.vector.tensor_copy(out=o, in_=i)
+            st["bg", g, h] = grp
+
+        def basis_quant(g, h):
+            quantize(ba_codes[g][h], ba_scl[g][h], st["bg", g, h][:, : CH[h][1]].rearrange("p n t -> p (n t)"))
+
+        def widen(n, a=0, b=16):
+            if a == 0:
+                wt = work.tile([128, 2048], BF16, name="br_wide", align_bytes=64, bufs=WIDE_BUFS)
+                st["wd", n] = wt
+            wide = st["wd", n]
+            raw = br_raw[n // 2][:, n % 2, :]
+            for j in range(a, b):
+                cols = slice(128 * j, 128 * j + 128)
+                scale = br_sc[:, n // 4, j : j + 1]
+                if j < WIDE_S.get(n, 0):
+                    nc.scalar.activation(out=wide[:, cols], in_=raw[:, cols].bitcast(E4M3), func=ACT.Copy, scale=scale)
+                elif CONTIG:
+                    nc.vector.tensor_scalar(
+                        out=wide[:, 512 * (j // 4) : 512 * (j // 4) + 512].rearrange("p (u m e) -> p m u e", u=2, e=2)[:, 32 * (j % 4) : 32 * (j % 4) + 32],
+                        in0=raw[:, cols].bitcast(E4M3).rearrange("p (m u e) -> p m u e", u=2, e=2), scalar1=scale, scalar2=None, op0=MULT)
+                else:
+                    nc.vector.tensor_scalar(out=wide[:, cols], in0=raw[:, cols].bitcast(E4M3), scalar1=scale, scalar2=None, op0=MULT)
+
+        def br_turn(n):
+            grp = work.tile([128, 2048], BF16, name="br_grp", align_bytes=64, bufs=3)
+            turn(st["wd", n][:].bitcast(F32), grp[:].bitcast(F32), CONTIG and n not in WIDE_S, ("b", n) in EXIT_V)
+            st["brg", n] = grp
+
+        def br_quant(n):
+            quantize(br_codes[n], br_scl[n], st["brg", n][:])
+
+        out_view = out.rearrange("(c p r) q -> c r p q", c=3, r=4)
+
+        def product(n, h):
+            s, w = CH[h]
+            acc = ps_acc.tile([128, 512], F32, name="acc")
+            for g in range(4):
+                cols = slice(128 * g, 128 * g + 128)
+                nc.tensor.matmul_mx(
+                    out=acc[:, :w],
+                    lhsT=br_codes[n][:, cols].bitcast(FP8X4),
+                    lhsT_scale=br_scl[n][:, cols],
+                    rhs=ba_codes[g][h][:].bitcast(FP8X4),
+                    rhs_scale=ba_scl[g][h][:],
+                    start=(g == 0),
+                    stop=(g == 3),
+                )
+            res = work.tile([128, 512], F32, name="res", align_bytes=64, bufs=RES_BUFS)
+            if (n, h) in OUT_V:
+                nc.vector.tensor_scalar(out=res[:, :w], in0=acc[:, :w], scalar1=c_bf[:, n // 4, n % 4 : n % 4 + 1], scalar2=None, op0=ADD)
+            else:
+                nc.scalar.activation(out=res[:, :w], in_=acc[:, :w], func=ACT.Identity, bias=c_bf[:, n // 4, n % 4 : n % 4 + 1])
+            nc.sync.dma_start(out=out_view[n // 4, n % 4][:, s : s + w], in_=res[:, :w])
+
+        def W(g):
+            w1_move(g), w1_widen(g), w1_quant(g)
+
+        def Y(h):
+            y_turn(h), y_quant(h)
+
+        def B(g, h):
+            basis_h(g, h), basis_gain(g, h), basis_inter(g, h), basis_quant(g, h)
+
+        def N(n):
+            br_turn(n), br_quant(n)
+
+        jobs = {"W": W, "Y": Y, "B": B, "N": N, "D": widen, "P": product, "wm": w1_move, "ww": w1_widen, "wq": w1_quant,
+                "yt": y_turn, "yq": y_quant, "bh": basis_h, "bg": basis_gain, "bi": basis_inter, "bq": basis_quant, "nt": br_turn, "nq": br_quant}
+        with ExitStack() as ctx2:
+            if MANUAL:
+                ctx2.enter_context(tc.manual_schedule())
+            for job in ORDER:
+                jobs[job[0]](*job[1:])

@@ -17,20 +17,19 @@ MULT = mybir.AluOpType.mult
 ACT = mybir.ActivationFunctionType
 
 
-CH = ((0, 512), (512, 256), (768, 256))
-WIDE_S = {0: 16, 1: 16, 2: 16, 3: 16}
-W1_S = ()
+CH = ((0, 512), (512, 512))
+SC = (0,)
 INTER_S = ()
 EXIT_V = ()
 OUT_V = ()
 ONEPASS = False
-CONTIG = True
 WIDE_BUFS = 4
+W4_BUFS = 6
 TH_BUFS = 3
 RES_BUFS = 6
-NTR, NH, NACC = 2, 3, 3
+NTR, NH, NACC = 3, 2, 3
 MANUAL = False
-ORDER = [('W', 0), ('Y', 0), ('B', 0, 0), ('W', 1), ('D', 0), ('B', 1, 0), ('W', 2), ('D', 1), ('B', 2, 0), ('W', 3), ('D', 2), ('B', 3, 0), ('N', 0), ('P', 0, 0), ('N', 1), ('P', 1, 0), ('D', 3), ('N', 2), ('P', 2, 0), ('D', 4), ('N', 3), ('P', 3, 0), ('D', 5), ('N', 4), ('P', 4, 0), ('Y', 1), ('B', 0, 1), ('D', 6), ('N', 5), ('P', 5, 0), ('B', 1, 1), ('D', 7), ('N', 6), ('P', 6, 0), ('B', 2, 1), ('D', 8), ('N', 7), ('P', 7, 0), ('B', 3, 1), ('P', 0, 1), ('P', 1, 1), ('P', 2, 1), ('D', 9), ('N', 8), ('P', 8, 0), ('Y', 2), ('B', 0, 2), ('P', 3, 1), ('P', 4, 1), ('P', 5, 1), ('D', 10), ('N', 9), ('P', 9, 0), ('B', 1, 2), ('P', 6, 1), ('P', 7, 1), ('P', 8, 1), ('D', 11), ('N', 10), ('P', 10, 0), ('B', 2, 2), ('P', 9, 1), ('P', 10, 1), ('N', 11), ('P', 11, 0), ('B', 3, 2), ('P', 11, 1), ('P', 0, 2), ('P', 1, 2), ('P', 2, 2), ('P', 3, 2), ('P', 4, 2), ('P', 5, 2), ('P', 6, 2), ('P', 7, 2), ('P', 8, 2), ('P', 9, 2), ('P', 10, 2), ('P', 11, 2)]
+ORDER = [('ww', 0), ('wi', 0), ('wq', 0), ('yt', 0), ('yq', 0), ('bh', 0, 0), ('bg', 0, 0), ('bi', 0, 0), ('bq', 0, 0), ('ww', 1), ('wi', 1), ('wq', 1), ('bh', 1, 0), ('bg', 1, 0), ('bi', 1, 0), ('bq', 1, 0), ('D', 0, 0, 4), ('D', 0, 4, 8), ('D', 0, 8, 12), ('D', 0, 12, 16), ('ww', 2), ('wi', 2), ('wq', 2), ('bh', 2, 0), ('bg', 2, 0), ('bi', 2, 0), ('bq', 2, 0), ('D', 1, 0, 4), ('D', 1, 4, 8), ('D', 1, 8, 12), ('D', 1, 12, 16), ('ww', 3), ('wi', 3), ('wq', 3), ('bh', 3, 0), ('bg', 3, 0), ('bi', 3, 0), ('bq', 3, 0), ('D', 2, 0, 4), ('D', 2, 4, 8), ('D', 2, 8, 12), ('D', 2, 12, 16), ('D', 3, 0, 4), ('D', 3, 4, 8), ('D', 3, 8, 12), ('D', 3, 12, 16), ('nt', 0, 0), ('nt', 0, 1), ('nq', 0), ('P', 0, 0), ('nt', 1, 0), ('nt', 1, 1), ('nq', 1), ('P', 1, 0), ('nt', 2, 0), ('nt', 2, 1), ('nq', 2), ('P', 2, 0), ('nt', 3, 0), ('nt', 3, 1), ('nq', 3), ('P', 3, 0), ('yt', 1), ('yq', 1), ('bh', 0, 1), ('bg', 0, 1), ('bi', 0, 1), ('bq', 0, 1), ('E', 1, 0), ('E', 1, 1), ('E', 1, 2), ('E', 1, 3), ('nt', 4, 0), ('nt', 4, 1), ('nq', 4), ('P', 4, 0), ('nt', 5, 0), ('nt', 5, 1), ('nq', 5), ('P', 5, 0), ('bh', 1, 1), ('bg', 1, 1), ('bi', 1, 1), ('bq', 1, 1), ('nt', 6, 0), ('nt', 6, 1), ('nq', 6), ('P', 6, 0), ('nt', 7, 0), ('nt', 7, 1), ('nq', 7), ('P', 7, 0), ('bh', 2, 1), ('bg', 2, 1), ('bi', 2, 1), ('bq', 2, 1), ('E', 2, 0), ('E', 2, 1), ('E', 2, 2), ('E', 2, 3), ('nt', 8, 0), ('nt', 8, 1), ('nq', 8), ('P', 8, 0), ('nt', 9, 0), ('nt', 9, 1), ('nq', 9), ('P', 9, 0), ('bh', 3, 1), ('bg', 3, 1), ('bi', 3, 1), ('bq', 3, 1), ('P', 0, 1), ('P', 1, 1), ('P', 2, 1), ('P', 3, 1), ('P', 4, 1), ('P', 5, 1), ('P', 6, 1), ('P', 7, 1), ('P', 8, 1), ('P', 9, 1), ('nt', 10, 0), ('nt', 10, 1), ('nq', 10), ('P', 10, 0), ('P', 10, 1), ('nt', 11, 0), ('nt', 11, 1), ('nq', 11), ('P', 11, 0), ('P', 11, 1)]
 
 
 def tile_operator_net_trunk_branch_d7_kernel(tc, y, b1, gain, c, w1_bytes, w1_scale, branch_bytes, branch_scale, out):
@@ -44,25 +43,31 @@ def tile_operator_net_trunk_branch_d7_kernel(tc, y, b1, gain, c, w1_bytes, w1_sc
 
         w1_raw = []
         for g in range(4):
-            w1_raw.append(keep.tile([128, 4, 512], U8, name=f"w1_raw{g}", align_bytes=64))
+            w1_raw.append(keep.tile([128, 4, 4, 128], U8, name=f"w1_raw{g}", align_bytes=64))
         y_sb = []
         for h in range(2):
             y_sb.append(keep.tile([128, 4, 512], BF16, name=f"y_sb{h}", align_bytes=64))
         br_raw = []
-        for d in range(6):
-            br_raw.append(keep.tile([128, 2, 2048], U8, name=f"br_raw{d}", align_bytes=64))
+        if SC:
+            for d in range(2):
+                br_raw.append(keep.tile([128, 2, 2048], U8, name=f"br_raw{d}", align_bytes=64))
+        br_blk = {}
+        for cc in range(len(SC), 3):
+            br_blk[cc] = keep.tile([128, 4, 4, 4, 128], U8, name=f"br_blk{cc}", align_bytes=64)
+        blk_view = branch_bytes.rearrange("(c p r) (b k) -> c r p b k", c=3, r=4, k=128)
         w1_sc = keep.tile([128, 16], F32, name="w1_sc")
         br_sc = keep.tile([128, 3, 16], F32, name="br_sc")
         b1_bf = keep.tile([128, 4, 4], BF16, name="b1_bf")
         gain_bf = keep.tile([128, 4, 4], BF16, name="gain_bf")
         c_bf = keep.tile([128, 3, 4], BF16, name="c_bf")
 
-        w1_view = w1_bytes.rearrange("(p k) n -> p k n", k=4)
+        w1_view = w1_bytes.rearrange("(p k) (g j n) -> g j p k n", k=4, g=4, j=4)
         y_view = y.rearrange("(h i p) k -> h p i k", h=2, p=128)
         br_view = branch_bytes.rearrange("(c p d r) k -> c d p r k", c=3, d=2, r=2)
 
         def load_w1(g):
-            nc.sync.dma_start(out=w1_raw[g][:], in_=w1_view[:, :, 512 * g : 512 * g + 512])
+            for j in range(4):
+                nc.sync.dma_start(out=w1_raw[g][:, j], in_=w1_view[g, j])
 
         ident = keep.tile([128, 128], F32, name="ident", align_bytes=64)
         make_identity(nc, ident[:])
@@ -81,12 +86,16 @@ def tile_operator_net_trunk_branch_d7_kernel(tc, y, b1, gain, c, w1_bytes, w1_sc
         for q in range(4):
             nc.gpsimd.dma_start(out=br_sc[32 * q : 32 * q + 32, :, :], in_=scale_view[q].partition_broadcast(32))
         nc.gpsimd.dma_start(out=c_bf[:], in_=c.rearrange("(c p r) -> p c r", c=3, r=4))
-        nc.sync.dma_start(out=br_raw[0][:], in_=br_view[0, 0])
+        if SC:
+            nc.sync.dma_start(out=br_raw[0][:], in_=br_view[0, 0])
         load_w1(2)
         load_w1(3)
         nc.sync.dma_start(out=y_sb[1][:], in_=y_view[1])
-        for d in range(1, 6):
-            nc.sync.dma_start(out=br_raw[d][:], in_=br_view[d // 2, d % 2])
+        if SC:
+            nc.sync.dma_start(out=br_raw[1][:], in_=br_view[0, 1])
+        for cc in range(len(SC), 3):
+            for r in range(4):
+                nc.sync.dma_start(out=br_blk[cc][:, :, :, r, :].rearrange("p g j k -> p (g j) k"), in_=blk_view[cc, r])
 
         w1_codes = [keep.tile([128, 512], U32, name=f"w1_codes{g}", align_bytes=64) for g in range(4)]
         w1_scl = [keep.tile([128, 512], U8, name=f"w1_scl{g}", align_bytes=64) for g in range(4)]
@@ -101,50 +110,42 @@ def tile_operator_net_trunk_branch_d7_kernel(tc, y, b1, gain, c, w1_bytes, w1_sc
         def quantize(codes, scl, src):
             nc.vector.quantize_mx(out=codes[:].bitcast(FP8X4), scales=scl[:], in_=src)
 
-        def w1_move(g):
-            inter = work.tile([128, 4, 4, 32, 4], U8, name="w1_inter", align_bytes=64)
-            src = w1_raw[g][:].rearrange("p k (j m t) -> p j t m k", j=4, t=4)
-            for j in range(4):
-                nc.vector.tensor_copy(out=inter[:, j], in_=src[:, j])
-            st["wi", g] = inter
-
         def w1_widen(g):
-            inter = st["wi", g]
-            wide = work.tile([128, 2048], BF16, name="w1_wide", align_bytes=64)
-            dst = wide[:].rearrange("p (t j x) -> p j t x", t=4, j=4)
+            wide = work.tile([128, 4, 512], BF16, name="w1_wide", align_bytes=64)
             for j in range(4):
-                fp8 = inter[:, j].rearrange("p t m k -> p t (m k)").bitcast(E4M3)
-                scale = w1_sc[:, 4 * g + j : 4 * g + j + 1]
-                if g in W1_S:
-                    for t in range(4):
-                        nc.scalar.activation(out=dst[:, j, t], in_=fp8[:, t], func=ACT.Copy, scale=scale)
-                else:
-                    nc.vector.tensor_scalar(out=dst[:, j], in0=fp8, scalar1=scale, scalar2=None, op0=MULT)
-            st["ww", g] = wide
+                nc.vector.tensor_scalar(
+                    out=wide[:, :, 128 * j : 128 * j + 128], in0=w1_raw[g][:, j].bitcast(E4M3), scalar1=w1_sc[:, 4 * g + j : 4 * g + j + 1], scalar2=None, op0=MULT)
+            st["wi", g] = wide
+
+        def w1_inter(g):
+            grp = work.tile([128, 2048], BF16, name="w1_grp", align_bytes=64)
+            nc.vector.tensor_copy(
+                out=grp[:].rearrange("p (t m k) -> p t m k", t=4, k=4),
+                in_=st["wi", g][:].rearrange("p k (m t) -> p t m k", t=4))
+            st["ww", g] = grp
 
         def w1_quant(g):
             quantize(w1_codes[g], w1_scl[g], st["ww", g][:])
 
-        def turn(words, dst_words, contiguous, on_vector):
-            for b in range(words.shape[1] // 512):
-                bank = ps_tr.tile([128, 4, 128], F32, name="tr")
-                for i in range(2):
-                    base = 256 * (2 * b + i)
-                    for u in range(2):
-                        src = words[:, base + 128 * u : base + 128 * u + 128] if contiguous else words[:, base + u : base + 256 : 2]
-                        nc.tensor.transpose(bank[:, 2 * i + u, :], src, ident[:])
-                o = dst_words[:, 512 * b : 512 * b + 512].rearrange("p (i r u) -> p i r u", i=2, u=2)
-                s = bank[:].rearrange("p (i u) r -> p i r u", i=2)
-                if on_vector:
-                    nc.vector.tensor_copy(out=o, in_=s)
-                else:
-                    nc.scalar.copy(out=o, in_=s)
+        def turn_bank(srcs, dst, on_vector):
+            bank = ps_tr.tile([128, 4, 128], F32, name="tr")
+            for i in range(2):
+                for u in range(2):
+                    nc.tensor.transpose(bank[:, 2 * i + u, :], srcs[i][:, u:256:2], ident[:])
+            o = dst.rearrange("p (i r u) -> p i r u", i=2, u=2)
+            s = bank[:].rearrange("p (i u) r -> p i r u", i=2)
+            if on_vector:
+                nc.vector.tensor_copy(out=o, in_=s)
+            else:
+                nc.scalar.copy(out=o, in_=s)
 
         def y_turn(h):
             s, w = CH[h]
-            words = y_sb[s // 512][:, (s % 512) // 128 : (s % 512 + w) // 128].rearrange("p i k -> p (i k)").bitcast(F32)
             grp = work.tile([128, 2048], BF16, name="y_grp", align_bytes=64)
-            turn(words, grp[:, : 4 * w].bitcast(F32), False, ("y", h) in EXIT_V)
+            for b in range(w // 256):
+                first = (s % 512) // 128 + 2 * b
+                srcs = [y_sb[s // 512][:, first + i, :].bitcast(F32) for i in range(2)]
+                turn_bank(srcs, grp[:, 1024 * b : 1024 * b + 1024].bitcast(F32), ("y", h) in EXIT_V)
             st["yg", h] = grp
 
         def y_quant(h):
@@ -190,7 +191,8 @@ def tile_operator_net_trunk_branch_d7_kernel(tc, y, b1, gain, c, w1_bytes, w1_sc
                 return
             s, w = CH[h]
             grp = work.tile([128, 512, 4], BF16, name="ba_grp", align_bytes=64)
-            o, i = grp[:, :w], st["bp", g, h][:, :, :w].rearrange("p t n -> p n t")
+            o = grp[:, :w].rearrange("p (c i) t -> p c t i", i=4)
+            i = st["bp", g, h][:, :, :w].rearrange("p t (c i) -> p c t i", i=4)
             if (g, h) in INTER_S:
                 nc.scalar.copy(out=o, in_=i)
             else:
@@ -209,19 +211,25 @@ def tile_operator_net_trunk_branch_d7_kernel(tc, y, b1, gain, c, w1_bytes, w1_sc
             for j in range(a, b):
                 cols = slice(128 * j, 128 * j + 128)
                 scale = br_sc[:, n // 4, j : j + 1]
-                if j < WIDE_S.get(n, 0):
-                    nc.scalar.activation(out=wide[:, cols], in_=raw[:, cols].bitcast(E4M3), func=ACT.Copy, scale=scale)
-                elif CONTIG:
-                    nc.vector.tensor_scalar(
-                        out=wide[:, 512 * (j // 4) : 512 * (j // 4) + 512].rearrange("p (u m e) -> p m u e", u=2, e=2)[:, 32 * (j % 4) : 32 * (j % 4) + 32],
-                        in0=raw[:, cols].bitcast(E4M3).rearrange("p (m u e) -> p m u e", u=2, e=2), scalar1=scale, scalar2=None, op0=MULT)
-                else:
-                    nc.vector.tensor_scalar(out=wide[:, cols], in0=raw[:, cols].bitcast(E4M3), scalar1=scale, scalar2=None, op0=MULT)
+                nc.scalar.activation(out=wide[:, cols], in_=raw[:, cols].bitcast(E4M3), func=ACT.Copy, scale=scale)
 
-        def br_turn(n):
-            grp = work.tile([128, 2048], BF16, name="br_grp", align_bytes=64, bufs=3)
-            turn(st["wd", n][:].bitcast(F32), grp[:].bitcast(F32), CONTIG and n not in WIDE_S, ("b", n) in EXIT_V)
-            st["brg", n] = grp
+        def widen4(cc, g):
+            wide = work.tile([128, 4, 512], BF16, name="br_wide4", align_bytes=64, bufs=W4_BUFS)
+            for j in range(4):
+                nc.vector.tensor_scalar(
+                    out=wide[:, :, 128 * j : 128 * j + 128], in0=br_blk[cc][:, g, j].bitcast(E4M3), scalar1=br_sc[:, cc, 4 * g + j : 4 * g + j + 1], scalar2=None, op0=MULT)
+            st["w4", cc, g] = wide
+
+        def br_turn(n, b):
+            if b == 0:
+                gt = work.tile([128, 2048], BF16, name="br_grp", align_bytes=64, bufs=3)
+                st["brg", n] = gt
+            dst = st["brg", n][:, 1024 * b : 1024 * b + 1024].bitcast(F32)
+            if n // 4 in SC:
+                srcs = [st["wd", n][:, 1024 * b + 512 * i : 1024 * b + 512 * i + 512].bitcast(F32) for i in range(2)]
+            else:
+                srcs = [st["w4", n // 4, 2 * b + i][:, n % 4].bitcast(F32) for i in range(2)]
+            turn_bank(srcs, dst, ("b", n) in EXIT_V)
 
         def br_quant(n):
             quantize(br_codes[n], br_scl[n], st["brg", n][:])
@@ -249,20 +257,8 @@ def tile_operator_net_trunk_branch_d7_kernel(tc, y, b1, gain, c, w1_bytes, w1_sc
                 nc.scalar.activation(out=res[:, :w], in_=acc[:, :w], func=ACT.Identity, bias=c_bf[:, n // 4, n % 4 : n % 4 + 1])
             nc.sync.dma_start(out=out_view[n // 4, n % 4][:, s : s + w], in_=res[:, :w])
 
-        def W(g):
-            w1_move(g), w1_widen(g), w1_quant(g)
-
-        def Y(h):
-            y_turn(h), y_quant(h)
-
-        def B(g, h):
-            basis_h(g, h), basis_gain(g, h), basis_inter(g, h), basis_quant(g, h)
-
-        def N(n):
-            br_turn(n), br_quant(n)
-
-        jobs = {"W": W, "Y": Y, "B": B, "N": N, "D": widen, "P": product, "wm": w1_move, "ww": w1_widen, "wq": w1_quant,
-                "yt": y_turn, "yq": y_quant, "bh": basis_h, "bg": basis_gain, "bi": basis_inter, "bq": basis_quant, "nt": br_turn, "nq": br_quant}
+        jobs = {"ww": w1_widen, "wi": w1_inter, "wq": w1_quant, "yt": y_turn, "yq": y_quant, "bh": basis_h, "bg": basis_gain, "bi": basis_inter,
+                "bq": basis_quant, "D": widen, "E": widen4, "nt": br_turn, "nq": br_quant, "P": product}
         with ExitStack() as ctx2:
             if MANUAL:
                 ctx2.enter_context(tc.manual_schedule())

from contextlib import ExitStack

import concourse.mybir as mybir
from concourse.masks import make_identity

Q, K, NB, S = 1024, 512, 2048, 1536
FLOPS = 2 * Q * K * NB + 2 * S * Q * NB

F32 = mybir.dt.float32
BF16 = mybir.dt.bfloat16
U32 = mybir.dt.uint32
U8 = mybir.dt.uint8
E4M3 = mybir.dt.float8_e4m3fn
FP8X4 = mybir.dt.float8_e4m3fn_x4
ADD = mybir.AluOpType.add
MULT = mybir.AluOpType.mult
ACT = mybir.ActivationFunctionType


CH = ((0, 512), (512, 512))
SC = (0,)
INTER_S = ()
EXIT_V = ()
OUT_V = ()
ONEPASS = False
WIDE_BUFS = 4
W4_BUFS = 6
TH_BUFS = 3
RES_BUFS = 6
NTR, NH, NACC = 3, 2, 3
MANUAL = False
ORDER = [('ww', 0), ('wi', 0), ('wq', 0), ('yt', 0), ('yq', 0), ('bh', 0, 0), ('bg', 0, 0), ('bi', 0, 0), ('bq', 0, 0), ('ww', 1), ('wi', 1), ('wq', 1), ('bh', 1, 0), ('bg', 1, 0), ('bi', 1, 0), ('bq', 1, 0), ('D', 0, 0, 4), ('D', 0, 4, 8), ('D', 0, 8, 12), ('D', 0, 12, 16), ('ww', 2), ('wi', 2), ('wq', 2), ('bh', 2, 0), ('bg', 2, 0), ('bi', 2, 0), ('bq', 2, 0), ('D', 1, 0, 4), ('D', 1, 4, 8), ('D', 1, 8, 12), ('D', 1, 12, 16), ('ww', 3), ('wi', 3), ('wq', 3), ('bh', 3, 0), ('bg', 3, 0), ('bi', 3, 0), ('bq', 3, 0), ('D', 2, 0, 4), ('D', 2, 4, 8), ('D', 2, 8, 12), ('D', 2, 12, 16), ('D', 3, 0, 4), ('D', 3, 4, 8), ('D', 3, 8, 12), ('D', 3, 12, 16), ('nt', 0, 0), ('nt', 0, 1), ('nq', 0), ('P', 0, 0), ('nt', 1, 0), ('nt', 1, 1), ('nq', 1), ('P', 1, 0), ('nt', 2, 0), ('nt', 2, 1), ('nq', 2), ('P', 2, 0), ('nt', 3, 0), ('nt', 3, 1), ('nq', 3), ('P', 3, 0), ('yt', 1), ('yq', 1), ('bh', 0, 1), ('bg', 0, 1), ('bi', 0, 1), ('bq', 0, 1), ('E', 1, 0), ('E', 1, 1), ('E', 1, 2), ('E', 1, 3), ('nt', 4, 0), ('nt', 4, 1), ('nq', 4), ('P', 4, 0), ('nt', 5, 0), ('nt', 5, 1), ('nq', 5), ('P', 5, 0), ('bh', 1, 1), ('bg', 1, 1), ('bi', 1, 1), ('bq', 1, 1), ('nt', 6, 0), ('nt', 6, 1), ('nq', 6), ('P', 6, 0), ('nt', 7, 0), ('nt', 7, 1), ('nq', 7), ('P', 7, 0), ('bh', 2, 1), ('bg', 2, 1), ('bi', 2, 1), ('bq', 2, 1), ('E', 2, 0), ('E', 2, 1), ('E', 2, 2), ('E', 2, 3), ('nt', 8, 0), ('nt', 8, 1), ('nq', 8), ('P', 8, 0), ('nt', 9, 0), ('nt', 9, 1), ('nq', 9), ('P', 9, 0), ('bh', 3, 1), ('bg', 3, 1), ('bi', 3, 1), ('bq', 3, 1), ('P', 0, 1), ('P', 1, 1), ('P', 2, 1), ('P', 3, 1), ('P', 4, 1), ('P', 5, 1), ('P', 6, 1), ('P', 7, 1), ('P', 8, 1), ('P', 9, 1), ('nt', 10, 0), ('nt', 10, 1), ('nq', 10), ('P', 10, 0), ('P', 10, 1), ('nt', 11, 0), ('nt', 11, 1), ('nq', 11), ('P', 11, 0), ('P', 11, 1)]


def tile_operator_net_trunk_branch_d7_kernel(tc, y, b1, gain, c, w1_bytes, w1_scale, branch_bytes, branch_scale, out):
    nc = tc.nc
    with ExitStack() as ctx:
        keep = ctx.enter_context(tc.tile_pool(name="keep", bufs=1))
        work = ctx.enter_context(tc.tile_pool(name="work", bufs=2))
        ps_tr = ctx.enter_context(tc.psum_pool(name="ps_tr", bufs=NTR))
        ps_h = ctx.enter_context(tc.psum_pool(name="ps_h", bufs=NH))
        ps_acc = ctx.enter_context(tc.psum_pool(name="ps_acc", bufs=NACC))

        w1_raw = []
        for g in range(4):
            w1_raw.append(keep.tile([128, 4, 4, 128], U8, name=f"w1_raw{g}", align_bytes=64))
        y_sb = []
        for h in range(2):
            y_sb.append(keep.tile([128, 4, 512], BF16, name=f"y_sb{h}", align_bytes=64))
        br_raw = []
        if SC:
            for d in range(2):
                br_raw.append(keep.tile([128, 2, 2048], U8, name=f"br_raw{d}", align_bytes=64))
        br_blk = {}
        for cc in range(len(SC), 3):
            br_blk[cc] = keep.tile([128, 4, 4, 4, 128], U8, name=f"br_blk{cc}", align_bytes=64)
        blk_view = branch_bytes.rearrange("(c p r) (b k) -> c r p b k", c=3, r=4, k=128)
        w1_sc = keep.tile([128, 16], F32, name="w1_sc")
        br_sc = keep.tile([128, 3, 16], F32, name="br_sc")
        b1_bf = keep.tile([128, 4, 4], BF16, name="b1_bf")
        gain_bf = keep.tile([128, 4, 4], BF16, name="gain_bf")
        c_bf = keep.tile([128, 3, 4], BF16, name="c_bf")

        w1_view = w1_bytes.rearrange("(p k) (g j n) -> g j p k n", k=4, g=4, j=4)
        y_view = y.rearrange("(h i p) k -> h p i k", h=2, p=128)
        br_view = branch_bytes.rearrange("(c p d r) k -> c d p r k", c=3, d=2, r=2)

        def load_w1(g):
            for j in range(4):
                nc.sync.dma_start(out=w1_raw[g][:, j], in_=w1_view[g, j])

        ident = keep.tile([128, 128], F32, name="ident", align_bytes=64)
        make_identity(nc, ident[:])
        warm = keep.tile([128, 1], F32, name="warm")
        nc.vector.memset(warm[:], 0.0)

        for q in range(4):
            nc.scalar.dma_start(out=w1_sc[32 * q : 32 * q + 32, :], in_=w1_scale[q].partition_broadcast(32))
        load_w1(0)
        nc.sync.dma_start(out=y_sb[0][:], in_=y_view[0])
        nc.scalar.activation(out=warm[:], in_=warm[:], func=ACT.Tanh)
        load_w1(1)
        nc.sync.dma_start(out=b1_bf[:], in_=b1.rearrange("(g p t) -> p g t", g=4, t=4))
        nc.sync.dma_start(out=gain_bf[:], in_=gain.rearrange("(g p t) -> p g t", g=4, t=4))
        scale_view = branch_scale.rearrange("(c q) j -> q c j", q=4)
        for q in range(4):
            nc.gpsimd.dma_start(out=br_sc[32 * q : 32 * q + 32, :, :], in_=scale_view[q].partition_broadcast(32))
        nc.gpsimd.dma_start(out=c_bf[:], in_=c.rearrange("(c p r) -> p c r", c=3, r=4))
        if SC:
            nc.sync.dma_start(out=br_raw[0][:], in_=br_view[0, 0])
        load_w1(2)
        load_w1(3)
        nc.sync.dma_start(out=y_sb[1][:], in_=y_view[1])
        if SC:
            nc.sync.dma_start(out=br_raw[1][:], in_=br_view[0, 1])
        for cc in range(len(SC), 3):
            for r in range(4):
                nc.sync.dma_start(out=br_blk[cc][:, :, :, r, :].rearrange("p g j k -> p (g j) k"), in_=blk_view[cc, r])

        w1_codes = [keep.tile([128, 512], U32, name=f"w1_codes{g}", align_bytes=64) for g in range(4)]
        w1_scl = [keep.tile([128, 512], U8, name=f"w1_scl{g}", align_bytes=64) for g in range(4)]
        y_codes = [keep.tile([128, w], U32, name=f"y_codes{h}", align_bytes=64) for h, (s, w) in enumerate(CH)]
        y_scl = [keep.tile([128, w], U8, name=f"y_scl{h}", align_bytes=64) for h, (s, w) in enumerate(CH)]
        ba_codes = [[keep.tile([128, w], U32, name=f"ba_codes{g}_{h}", align_bytes=64) for h, (s, w) in enumerate(CH)] for g in range(4)]
        ba_scl = [[keep.tile([128, w], U8, name=f"ba_scl{g}_{h}", align_bytes=64) for h, (s, w) in enumerate(CH)] for g in range(4)]
        br_codes = [keep.tile([128, 512], U32, name=f"br_codes{n}", align_bytes=64) for n in range(12)]
        br_scl = [keep.tile([128, 512], U8, name=f"br_scl{n}", align_bytes=64) for n in range(12)]
        st = {}

        def quantize(codes, scl, src):
            nc.vector.quantize_mx(out=codes[:].bitcast(FP8X4), scales=scl[:], in_=src)

        def w1_widen(g):
            wide = work.tile([128, 4, 512], BF16, name="w1_wide", align_bytes=64)
            for j in range(4):
                nc.vector.tensor_scalar(
                    out=wide[:, :, 128 * j : 128 * j + 128], in0=w1_raw[g][:, j].bitcast(E4M3), scalar1=w1_sc[:, 4 * g + j : 4 * g + j + 1], scalar2=None, op0=MULT)
            st["wi", g] = wide

        def w1_inter(g):
            grp = work.tile([128, 2048], BF16, name="w1_grp", align_bytes=64)
            nc.vector.tensor_copy(
                out=grp[:].rearrange("p (t m k) -> p t m k", t=4, k=4),
                in_=st["wi", g][:].rearrange("p k (m t) -> p t m k", t=4))
            st["ww", g] = grp

        def w1_quant(g):
            quantize(w1_codes[g], w1_scl[g], st["ww", g][:])

        def turn_bank(srcs, dst, on_vector):
            bank = ps_tr.tile([128, 4, 128], F32, name="tr")
            for i in range(2):
                for u in range(2):
                    nc.tensor.transpose(bank[:, 2 * i + u, :], srcs[i][:, u:256:2], ident[:])
            o = dst.rearrange("p (i r u) -> p i r u", i=2, u=2)
            s = bank[:].rearrange("p (i u) r -> p i r u", i=2)
            if on_vector:
                nc.vector.tensor_copy(out=o, in_=s)
            else:
                nc.scalar.copy(out=o, in_=s)

        def y_turn(h):
            s, w = CH[h]
            grp = work.tile([128, 2048], BF16, name="y_grp", align_bytes=64)
            for b in range(w // 256):
                first = (s % 512) // 128 + 2 * b
                srcs = [y_sb[s // 512][:, first + i, :].bitcast(F32) for i in range(2)]
                turn_bank(srcs, grp[:, 1024 * b : 1024 * b + 1024].bitcast(F32), ("y", h) in EXIT_V)
            st["yg", h] = grp

        def y_quant(h):
            quantize(y_codes[h], y_scl[h], st["yg", h][:, : 4 * CH[h][1]])

        def basis_h(g, h):
            s, w = CH[h]
            th = work.tile([128, 4, 512], F32, name="th", align_bytes=64, bufs=TH_BUFS)
            for t in range(4):
                acc = ps_h.tile([128, 512], F32, name="h_ps")
                cols = slice(128 * t, 128 * t + 128)
                nc.tensor.matmul_mx(
                    out=acc[:, :w],
                    lhsT=w1_codes[g][:, cols].bitcast(FP8X4),
                    lhsT_scale=w1_scl[g][:, cols],
                    rhs=y_codes[h][:].bitcast(FP8X4),
                    rhs_scale=y_scl[h][:],
                    start=True,
                    stop=True,
                )
                nc.scalar.activation(out=th[:, t, :w], in_=acc[:, :w], func=ACT.Tanh, bias=b1_bf[:, g, t : t + 1])
            st["th", g, h] = th

        def basis_gain(g, h):
            s, w = CH[h]
            th = st["th", g, h]
            if ONEPASS:
                grp = work.tile([128, 512, 4], BF16, name="ba_grp", align_bytes=64)
                nc.vector.tensor_tensor(
                    out=grp[:, :w], in0=th[:, :, :w].rearrange("p t n -> p n t"),
                    in1=gain_bf[:, g, :].unsqueeze(1).to_broadcast([128, w, 4]), op=MULT)
                st["bg", g, h] = grp
                return
            planes = work.tile([128, 4, 512], BF16, name="planes", align_bytes=64)
            for t in range(4):
                nc.vector.tensor_scalar(
                    out=planes[:, t, :w], in0=th[:, t, :w], scalar1=gain_bf[:, g, t : t + 1], scalar2=None, op0=MULT
                )
            st["bp", g, h] = planes

        def basis_inter(g, h):
            if ONEPASS:
                return
            s, w = CH[h]
            grp = work.tile([128, 512, 4], BF16, name="ba_grp", align_bytes=64)
            o = grp[:, :w].rearrange("p (c i) t -> p c t i", i=4)
            i = st["bp", g, h][:, :, :w].rearrange("p t (c i) -> p c t i", i=4)
            if (g, h) in INTER_S:
                nc.scalar.copy(out=o, in_=i)
            else:
                nc.vector.tensor_copy(out=o, in_=i)
            st["bg", g, h] = grp

        def basis_quant(g, h):
            quantize(ba_codes[g][h], ba_scl[g][h], st["bg", g, h][:, : CH[h][1]].rearrange("p n t -> p (n t)"))

        def widen(n, a=0, b=16):
            if a == 0:
                wt = work.tile([128, 2048], BF16, name="br_wide", align_bytes=64, bufs=WIDE_BUFS)
                st["wd", n] = wt
            wide = st["wd", n]
            raw = br_raw[n // 2][:, n % 2, :]
            for j in range(a, b):
                cols = slice(128 * j, 128 * j + 128)
                scale = br_sc[:, n // 4, j : j + 1]
                nc.scalar.activation(out=wide[:, cols], in_=raw[:, cols].bitcast(E4M3), func=ACT.Copy, scale=scale)

        def widen4(cc, g):
            wide = work.tile([128, 4, 512], BF16, name="br_wide4", align_bytes=64, bufs=W4_BUFS)
            for j in range(4):
                nc.vector.tensor_scalar(
                    out=wide[:, :, 128 * j : 128 * j + 128], in0=br_blk[cc][:, g, j].bitcast(E4M3), scalar1=br_sc[:, cc, 4 * g + j : 4 * g + j + 1], scalar2=None, op0=MULT)
            st["w4", cc, g] = wide

        def br_turn(n, b):
            if b == 0:
                gt = work.tile([128, 2048], BF16, name="br_grp", align_bytes=64, bufs=3)
                st["brg", n] = gt
            dst = st["brg", n][:, 1024 * b : 1024 * b + 1024].bitcast(F32)
            if n // 4 in SC:
                srcs = [st["wd", n][:, 1024 * b + 512 * i : 1024 * b + 512 * i + 512].bitcast(F32) for i in range(2)]
            else:
                srcs = [st["w4", n // 4, 2 * b + i][:, n % 4].bitcast(F32) for i in range(2)]
            turn_bank(srcs, dst, ("b", n) in EXIT_V)

        def br_quant(n):
            quantize(br_codes[n], br_scl[n], st["brg", n][:])

        out_view = out.rearrange("(c p r) q -> c r p q", c=3, r=4)

        def product(n, h):
            s, w = CH[h]
            acc = ps_acc.tile([128, 512], F32, name="acc")
            for g in range(4):
                cols = slice(128 * g, 128 * g + 128)
                nc.tensor.matmul_mx(
                    out=acc[:, :w],
                    lhsT=br_codes[n][:, cols].bitcast(FP8X4),
                    lhsT_scale=br_scl[n][:, cols],
                    rhs=ba_codes[g][h][:].bitcast(FP8X4),
                    rhs_scale=ba_scl[g][h][:],
                    start=(g == 0),
                    stop=(g == 3),
                )
            res = work.tile([128, 512], F32, name="res", align_bytes=64, bufs=RES_BUFS)
            if (n, h) in OUT_V:
                nc.vector.tensor_scalar(out=res[:, :w], in0=acc[:, :w], scalar1=c_bf[:, n // 4, n % 4 : n % 4 + 1], scalar2=None, op0=ADD)
            else:
                nc.scalar.activation(out=res[:, :w], in_=acc[:, :w], func=ACT.Identity, bias=c_bf[:, n // 4, n % 4 : n % 4 + 1])
            nc.sync.dma_start(out=out_view[n // 4, n % 4][:, s : s + w], in_=res[:, :w])

        jobs = {"ww": w1_widen, "wi": w1_inter, "wq": w1_quant, "yt": y_turn, "yq": y_quant, "bh": basis_h, "bg": basis_gain, "bi": basis_inter,
                "bq": basis_quant, "D": widen, "E": widen4, "nt": br_turn, "nq": br_quant, "P": product}
        with ExitStack() as ctx2:
            if MANUAL:
                ctx2.enter_context(tc.manual_schedule())
            for job in ORDER:
                jobs[job[0]](*job[1:])
